import numpy as np
CORES = [0,4,8,12,16,20,24,28,32,36,40,44,48,52,56,60,64,68,72,76,80,84,88,92,96,100,104,108,112,116,120,124,128,132,136,140,144,148,152,156,160,164,168,172,176,180,184,188,192,196,200,204,208,212,216,220,224,228,232,236,240,244,248,252,256,260,264,268,272,276,280,284,288,292,296,300,304,308,312,316,320,324,328,332,336,340,344,348,352,356,360,364,368,372,376,380]
N = 96
def setup_inputs(rng):
    return {"x": rng.standard_normal((N, 128, 512), dtype=np.float32)}
def reference(x):
    s = x.sum(axis=0, dtype=np.float64).astype(x.dtype)
    return {"y": np.broadcast_to(s, (N,) + s.shape)}

@@ -1,0 +1,136 @@
+from concourse.bass import RemoteDMATransfer, DstId
+
+SCRATCH = {
+    "buf": ("sbuf", [128, 1024], "float32"),
+}
+SEMAPHORES = ["loc", "sent", "m", "h", "o", "x1", "x2", "tot", "r", "d"]
+
+M = (2, 3, 6, 7)
+H = (2, 1, 6, 5)
+O = (1, 3, 5, 7)
+R = (3, 2, 7, 6)
+Q = (1, 1, 5, 5)
+
+XS, YB = 0, 512
+MB = 0
+QB = 0
+HB = 128
+OB = 320
+XB = 384
+TB = 392
+RB = 400
+
+
+def rank_program(g, core, T, topo):
+    host, chip, c = topo.host(core), topo.chip(core), core % 8
+    par, j = chip % 2, chip // 2
+    buf, sem = T.buf, T.sem
+    sent = [0]
+
+    def cid(h, k, cc):
+        return h * 128 + k * 8 + cc
+
+    def cols(a, n):
+        return buf[:, a:a + n]
+
+    def issue(ts):
+        out = []
+        for dsts, srcs, rsem, mask in ts:
+            ids = []
+            for d, ap in dsts:
+                rid, pid = topo.addr(d, core)
+                ids.append(DstId(rid=rid, pnc=pid))
+            out.append(RemoteDMATransfer(dst_ids=ids, dma_engine_mask=mask, remote_sem=rsem, srcs=list(srcs),
+                                         dsts=[ap for d, ap in dsts], alu_op=1 if len(srcs) > 1 else 0))
+            sent[0] += bin(mask).count("1")
+        g.remote_dma_fused(out, local_sem=sem.sent)
+
+    def finish():
+        if sent[0]:
+            g.wait_ge(sem.sent, sent[0])
+
+    if host == 3:
+        if c in O:
+            g.wait_ge(sem.x1, 2)
+            issue([([(cid(0, chip, c), cols(XB + 4, 4))], [cols(XB, 4)], sem.x2, 0x03)])
+            g.wait_ge(sem.x2, 2)
+            issue([([(cid(2, chip, c), cols(TB + 4, 4))], [cols(XB, 4), cols(XB + 4, 4)], sem.tot, 0x03)])
+            finish()
+        return
+
+    ranks = (cid(host, chip, 0), cid(host, chip, 4))
+
+    if c in (0, 4):
+        g.dma_start(cols(XS, 512), T.x[:]).then_inc(sem.loc, 16)
+        g.wait_ge(sem.loc, 16)
+        slot = 0 if c == 0 else 1
+        ts = []
+        for i in range(4):
+            ts.append(([(cid(host, chip, H[i]), cols(HB + 64 * slot, 64))],
+                       [cols(XS + 256 * par + 64 * i, 64)], sem.h, 0x3 << (4 * i)))
+            ts.append(([(cid(host, chip, M[i]), cols(MB + 64 * slot, 64))],
+                       [cols(XS + 256 * (1 - par) + 64 * i, 64)], sem.m, 0xC << (4 * i)))
+        issue(ts)
+        g.wait_ge(sem.d, 4 * 8 + 2 * 16)
+        g.dma_start(T.y[:], cols(YB, 512)).then_inc(sem.loc, 16)
+        g.wait_ge(sem.loc, 32)
+        finish()
+        return
+
+    if c in M:
+        i = M.index(c)
+        g.wait_ge(sem.m, 4)
+        issue([([(cid(host, chip ^ 1, H[i]), cols(HB + 128, 64))], [cols(MB, 64), cols(MB + 64, 64)], sem.h, 0xFF)])
+
+    if c in H:
+        i = H.index(c)
+        g.wait_ge(sem.h, 2 + 2 + 8)
+        issue([([(cid(host, 2 * jj + par, O[i]), cols(OB + 8 * j, 8))],
+                [cols(HB + 64 * s + 8 * jj, 8) for s in range(3)], sem.o, 1 << jj) for jj in range(8)])
+
+    if c in O:
+        i = O.index(c)
+        alpha = [cols(OB + 8 * s, 4) for s in range(8)]
+        beta = [cols(OB + 8 * s + 4, 4) for s in range(8)]
+        x0, x1 = cols(XB, 4), cols(XB + 4, 4)
+
+        def lane_receivers(off, n):
+            return [(cid(host, 2 * jj + par, R[i]), cols(RB + 8 * j + off, n)) for jj in range(8)]
+
+        g.wait_ge(sem.o, 8)
+        if host == 0:
+            issue([([(cid(1, chip, c), x0)], alpha, sem.x1, 0x03)])
+            g.wait_ge(sem.x1, 2)
+            issue([([(cid(3, chip, c), x1)], beta + [x0], sem.x2, 0x03)])
+            g.wait_ge(sem.x2, 2)
+            g.wait_ge(sem.tot, 2)
+            issue([(lane_receivers(4, 4), beta + [x0, x1], sem.r, 0x03),
+                   ([(cid(1, chip, c), cols(TB + 4, 4))], beta + [x0, x1], sem.tot, 0x0C),
+                   (lane_receivers(0, 4), [cols(TB, 4)], sem.r, 0x30)])
+        elif host == 1:
+            issue([([(cid(0, chip, c), x0)], beta, sem.x1, 0x03)])
+            g.wait_ge(sem.x1, 4)
+            issue([(lane_receivers(0, 4), alpha + [x0, x1], sem.r, 0x03),
+                   ([(cid(0, chip, c), cols(TB, 4)), (cid(2, chip, c), cols(TB, 4))], alpha + [x0, x1], sem.tot, 0x0C)])
+            g.wait_ge(sem.tot, 2)
+            issue([(lane_receivers(4, 4), [cols(TB + 4, 4)], sem.r, 0x03)])
+        else:
+            issue([([(cid(1, chip, c), x1)], alpha, sem.x1, 0x03),
+                   ([(cid(3, chip, c), x0)], beta, sem.x1, 0x0C)])
+            g.wait_ge(sem.tot, 4)
+            issue([(lane_receivers(0, 8), [cols(TB, 8)], sem.r, 0x03)])
+
+    if c in R:
+        i = R.index(c)
+        g.wait_ge(sem.r, 32 if host < 2 else 16)
+        lane = cols(YB + 256 * par + 64 * i, 64)
+        issue([([(ranks[0], lane), (ranks[1], lane), (cid(host, chip ^ 1, Q[i]), cols(QB + 64 * (i % 2), 64))],
+                [cols(RB, 64)], sem.d, 0xFF)])
+
+    if c in Q:
+        i = Q.index(c)
+        g.wait_ge(sem.d, 16)
+        lanes = cols(YB + 256 * (1 - par) + 64 * i, 128)
+        issue([([(ranks[0], lanes), (ranks[1], lanes)], [cols(QB, 128)], sem.d, 0xFFFF)])
+
+    finish()

@@ -1,7 +1,9 @@
 from concourse.bass import RemoteDMATransfer, DstId
 
 SCRATCH = {
-    "buf": ("sbuf", [128, 1024], "float32"),
+    "lane": ("dram", [16, 128, 64], "float32"),
+    "piece": ("dram", [32, 128, 8], "float32"),
+    "part": ("dram", [36, 128, 4], "float32"),
 }
 SEMAPHORES = ["loc", "sent", "m", "h", "o", "x1", "x2", "tot", "r", "d"]
 
@@ -11,27 +13,27 @@ O = (1, 3, 5, 7)
 R = (3, 2, 7, 6)
 Q = (1, 1, 5, 5)
 
-XS, YB = 0, 512
+XS, YB = 0, 8
 MB = 0
 QB = 0
-HB = 128
-OB = 320
-XB = 384
-TB = 392
-RB = 400
+HB = 2
+RL = 5
+HP = 0
+OB = 24
+OQ = 0
+XB = 16
+TB = 18
+RB = 20
 
 
 def rank_program(g, core, T, topo):
     host, chip, c = topo.host(core), topo.chip(core), core % 8
     par, j = chip % 2, chip // 2
-    buf, sem = T.buf, T.sem
-    sent = [0]
+    lane, piece, part, sem = T.lane, T.piece, T.part, T.sem
+    sent, loc = [0], [0]
 
     def cid(h, k, cc):
         return h * 128 + k * 8 + cc
-
-    def cols(a, n):
-        return buf[:, a:a + n]
 
     def issue(ts):
         out = []
@@ -45,6 +47,11 @@ def rank_program(g, core, T, topo):
             sent[0] += bin(mask).count("1")
         g.remote_dma_fused(out, local_sem=sem.sent)
 
+    def local(out, in_):
+        g.dma_start(out, in_).then_inc(sem.loc, 16)
+        loc[0] += 16
+        g.wait_ge(sem.loc, loc[0])
+
     def finish():
         if sent[0]:
             g.wait_ge(sem.sent, sent[0])
@@ -52,85 +59,85 @@ def rank_program(g, core, T, topo):
     if host == 3:
         if c in O:
             g.wait_ge(sem.x1, 2)
-            issue([([(cid(0, chip, c), cols(XB + 4, 4))], [cols(XB, 4)], sem.x2, 0x03)])
+            issue([([(cid(0, chip, c), part[XB + 1])], [part[XB]], sem.x2, 0x03)])
             g.wait_ge(sem.x2, 2)
-            issue([([(cid(2, chip, c), cols(TB + 4, 4))], [cols(XB, 4), cols(XB + 4, 4)], sem.tot, 0x03)])
+            issue([([(cid(2, chip, c), part[TB + 1])], [part[XB], part[XB + 1]], sem.tot, 0x03)])
             finish()
         return
 
     ranks = (cid(host, chip, 0), cid(host, chip, 4))
 
     if c in (0, 4):
-        g.dma_start(cols(XS, 512), T.x[:]).then_inc(sem.loc, 16)
-        g.wait_ge(sem.loc, 16)
+        local(lane[XS:XS + 8], T.x[:])
         slot = 0 if c == 0 else 1
         ts = []
         for i in range(4):
-            ts.append(([(cid(host, chip, H[i]), cols(HB + 64 * slot, 64))],
-                       [cols(XS + 256 * par + 64 * i, 64)], sem.h, 0x3 << (4 * i)))
-            ts.append(([(cid(host, chip, M[i]), cols(MB + 64 * slot, 64))],
-                       [cols(XS + 256 * (1 - par) + 64 * i, 64)], sem.m, 0xC << (4 * i)))
+            ts.append(([(cid(host, chip, H[i]), lane[HB + slot])], [lane[XS + 4 * par + i]], sem.h, 0x3 << (4 * i)))
+            ts.append(([(cid(host, chip, M[i]), lane[MB + slot])], [lane[XS + 4 * (1 - par) + i]], sem.m, 0xC << (4 * i)))
         issue(ts)
-        g.wait_ge(sem.d, 4 * 8 + 2 * 16)
-        g.dma_start(T.y[:], cols(YB, 512)).then_inc(sem.loc, 16)
-        g.wait_ge(sem.loc, 32)
+        g.wait_ge(sem.d, 8 * 8)
+        local(T.y[:], lane[YB:YB + 8])
         finish()
         return
 
     if c in M:
         i = M.index(c)
         g.wait_ge(sem.m, 4)
-        issue([([(cid(host, chip ^ 1, H[i]), cols(HB + 128, 64))], [cols(MB, 64), cols(MB + 64, 64)], sem.h, 0xFF)])
+        issue([([(cid(host, chip ^ 1, H[i]), lane[HB + 2])], [lane[MB], lane[MB + 1]], sem.h, 0xFF)])
 
     if c in H:
         i = H.index(c)
         g.wait_ge(sem.h, 2 + 2 + 8)
-        issue([([(cid(host, 2 * jj + par, O[i]), cols(OB + 8 * j, 8))],
-                [cols(HB + 64 * s + 8 * jj, 8) for s in range(3)], sem.o, 1 << jj) for jj in range(8)])
+        local(piece[HP:HP + 24], lane[HB:HB + 3])
+        issue([([(cid(host, 2 * jj + par, O[i]), piece[OB + j])],
+                [piece[HP + 8 * s + jj] for s in range(3)], sem.o, 1 << jj) for jj in range(8)])
 
     if c in O:
         i = O.index(c)
-        alpha = [cols(OB + 8 * s, 4) for s in range(8)]
-        beta = [cols(OB + 8 * s + 4, 4) for s in range(8)]
-        x0, x1 = cols(XB, 4), cols(XB + 4, 4)
+        alpha = [part[OQ + 2 * s] for s in range(8)]
+        beta = [part[OQ + 2 * s + 1] for s in range(8)]
+        x0, x1 = part[XB], part[XB + 1]
 
-        def lane_receivers(off, n):
-            return [(cid(host, 2 * jj + par, R[i]), cols(RB + 8 * j + off, n)) for jj in range(8)]
+        def lane_receivers(ab):
+            return [(cid(host, 2 * jj + par, R[i]), part[RB + 2 * j + ab]) for jj in range(8)]
 
         g.wait_ge(sem.o, 8)
+        local(part[OQ:OQ + 16], piece[OB:OB + 8])
         if host == 0:
             issue([([(cid(1, chip, c), x0)], alpha, sem.x1, 0x03)])
             g.wait_ge(sem.x1, 2)
             issue([([(cid(3, chip, c), x1)], beta + [x0], sem.x2, 0x03)])
             g.wait_ge(sem.x2, 2)
             g.wait_ge(sem.tot, 2)
-            issue([(lane_receivers(4, 4), beta + [x0, x1], sem.r, 0x03),
-                   ([(cid(1, chip, c), cols(TB + 4, 4))], beta + [x0, x1], sem.tot, 0x0C),
-                   (lane_receivers(0, 4), [cols(TB, 4)], sem.r, 0x30)])
+            issue([(lane_receivers(1), beta + [x0, x1], sem.r, 0x03),
+                   ([(cid(1, chip, c), part[TB + 1])], beta + [x0, x1], sem.tot, 0x0C),
+                   (lane_receivers(0), [part[TB]], sem.r, 0x30)])
         elif host == 1:
             issue([([(cid(0, chip, c), x0)], beta, sem.x1, 0x03)])
             g.wait_ge(sem.x1, 4)
-            issue([(lane_receivers(0, 4), alpha + [x0, x1], sem.r, 0x03),
-                   ([(cid(0, chip, c), cols(TB, 4)), (cid(2, chip, c), cols(TB, 4))], alpha + [x0, x1], sem.tot, 0x0C)])
+            issue([(lane_receivers(0), alpha + [x0, x1], sem.r, 0x03),
+                   ([(cid(0, chip, c), part[TB]), (cid(2, chip, c), part[TB])], alpha + [x0, x1], sem.tot, 0x0C)])
             g.wait_ge(sem.tot, 2)
-            issue([(lane_receivers(4, 4), [cols(TB + 4, 4)], sem.r, 0x03)])
+            issue([(lane_receivers(1), [part[TB + 1]], sem.r, 0x03)])
         else:
             issue([([(cid(1, chip, c), x1)], alpha, sem.x1, 0x03),
                    ([(cid(3, chip, c), x0)], beta, sem.x1, 0x0C)])
             g.wait_ge(sem.tot, 4)
-            issue([(lane_receivers(0, 8), [cols(TB, 8)], sem.r, 0x03)])
+            issue([(lane_receivers(0), [part[TB]], sem.r, 0x03),
+                   (lane_receivers(1), [part[TB + 1]], sem.r, 0x0C)])
 
     if c in R:
         i = R.index(c)
-        g.wait_ge(sem.r, 32 if host < 2 else 16)
-        lane = cols(YB + 256 * par + 64 * i, 64)
-        issue([([(ranks[0], lane), (ranks[1], lane), (cid(host, chip ^ 1, Q[i]), cols(QB + 64 * (i % 2), 64))],
-                [cols(RB, 64)], sem.d, 0xFF)])
+        g.wait_ge(sem.r, 8 * 2 * 2)
+        local(lane[RL], part[RB:RB + 16])
+        y = lane[YB + 4 * par + i]
+        issue([([(ranks[0], y), (ranks[1], y), (cid(host, chip ^ 1, Q[i]), lane[QB + i % 2])],
+                [lane[RL]], sem.d, 0xFF)])
 
     if c in Q:
         i = Q.index(c)
         g.wait_ge(sem.d, 16)
-        lanes = cols(YB + 256 * (1 - par) + 64 * i, 128)
-        issue([([(ranks[0], lanes), (ranks[1], lanes)], [cols(QB, 128)], sem.d, 0xFFFF)])
+        issue([([(r, lane[YB + 4 * (1 - par) + i + n]) for r in ranks], [lane[QB + n]], sem.d, 0xFF << (8 * n))
+               for n in range(2)])
 
     finish()

@@ -1,7 +1,7 @@
 from concourse.bass import RemoteDMATransfer, DstId
 
 SCRATCH = {
-    "lane": ("dram", [16, 128, 64], "float32"),
+    "lane": ("dram", [8, 128, 64], "float32"),
     "piece": ("dram", [32, 128, 8], "float32"),
     "part": ("dram", [36, 128, 4], "float32"),
 }
@@ -11,13 +11,13 @@ M = (2, 3, 6, 7)
 H = (2, 1, 6, 5)
 O = (1, 3, 5, 7)
 R = (3, 2, 7, 6)
-Q = (1, 1, 5, 5)
+Q = (1, 2, 5, 6)
 
-XS, YB = 0, 8
+XY = 0
 MB = 0
-QB = 0
 HB = 2
 RL = 5
+QB = 6
 HP = 0
 OB = 24
 OQ = 0
@@ -68,15 +68,15 @@ def rank_program(g, core, T, topo):
     ranks = (cid(host, chip, 0), cid(host, chip, 4))
 
     if c in (0, 4):
-        local(lane[XS:XS + 8], T.x[:])
+        local(lane[XY:XY + 8], T.x[:])
         slot = 0 if c == 0 else 1
         ts = []
         for i in range(4):
-            ts.append(([(cid(host, chip, H[i]), lane[HB + slot])], [lane[XS + 4 * par + i]], sem.h, 0x3 << (4 * i)))
-            ts.append(([(cid(host, chip, M[i]), lane[MB + slot])], [lane[XS + 4 * (1 - par) + i]], sem.m, 0xC << (4 * i)))
+            ts.append(([(cid(host, chip, H[i]), lane[HB + slot])], [lane[XY + 4 * par + i]], sem.h, 0x3 << (4 * i)))
+            ts.append(([(cid(host, chip, M[i]), lane[MB + slot])], [lane[XY + 4 * (1 - par) + i]], sem.m, 0xC << (4 * i)))
         issue(ts)
-        g.wait_ge(sem.d, 8 * 8)
-        local(T.y[:], lane[YB:YB + 8])
+        g.wait_ge(sem.d, 4 * 8 + 4 * 16)
+        local(T.y[:], lane[XY:XY + 8])
         finish()
         return
 
@@ -130,14 +130,13 @@ def rank_program(g, core, T, topo):
         i = R.index(c)
         g.wait_ge(sem.r, 8 * 2 * 2)
         local(lane[RL], part[RB:RB + 16])
-        y = lane[YB + 4 * par + i]
-        issue([([(ranks[0], y), (ranks[1], y), (cid(host, chip ^ 1, Q[i]), lane[QB + i % 2])],
+        y = lane[XY + 4 * par + i]
+        issue([([(ranks[0], y), (ranks[1], y), (cid(host, chip ^ 1, Q[i]), lane[QB])],
                 [lane[RL]], sem.d, 0xFF)])
 
     if c in Q:
         i = Q.index(c)
-        g.wait_ge(sem.d, 16)
-        issue([([(r, lane[YB + 4 * (1 - par) + i + n]) for r in ranks], [lane[QB + n]], sem.d, 0xFF << (8 * n))
-               for n in range(2)])
+        g.wait_ge(sem.d, 8)
+        issue([([(r, lane[XY + 4 * (1 - par) + i]) for r in ranks], [lane[QB]], sem.d, 0xFFFF)])
 
     finish()

from concourse.bass import RemoteDMATransfer, DstId

SCRATCH = {
    "lane": ("dram", [8, 128, 64], "float32"),
    "piece": ("dram", [32, 128, 8], "float32"),
    "part": ("dram", [36, 128, 4], "float32"),
}
SEMAPHORES = ["loc", "sent", "m", "h", "o", "x1", "x2", "tot", "r", "d"]

M = (2, 3, 6, 7)
H = (2, 1, 6, 5)
O = (1, 3, 5, 7)
R = (3, 2, 7, 6)
Q = (1, 2, 5, 6)

XY = 0
MB = 0
HB = 2
RL = 5
QB = 6
HP = 0
OB = 24
OQ = 0
XB = 16
TB = 18
RB = 20


def rank_program(g, core, T, topo):
    host, chip, c = topo.host(core), topo.chip(core), core % 8
    par, j = chip % 2, chip // 2
    lane, piece, part, sem = T.lane, T.piece, T.part, T.sem
    sent, loc = [0], [0]

    def cid(h, k, cc):
        return h * 128 + k * 8 + cc

    def issue(ts):
        out = []
        for dsts, srcs, rsem, mask in ts:
            ids = []
            for d, ap in dsts:
                rid, pid = topo.addr(d, core)
                ids.append(DstId(rid=rid, pnc=pid))
            out.append(RemoteDMATransfer(dst_ids=ids, dma_engine_mask=mask, remote_sem=rsem, srcs=list(srcs),
                                         dsts=[ap for d, ap in dsts], alu_op=1 if len(srcs) > 1 else 0))
            sent[0] += bin(mask).count("1")
        g.remote_dma_fused(out, local_sem=sem.sent)

    def local(out, in_):
        g.dma_start(out, in_).then_inc(sem.loc, 16)
        loc[0] += 16
        g.wait_ge(sem.loc, loc[0])

    def finish():
        if sent[0]:
            g.wait_ge(sem.sent, sent[0])

    if host == 3:
        if c in O:
            g.wait_ge(sem.x1, 2)
            issue([([(cid(0, chip, c), part[XB + 1])], [part[XB]], sem.x2, 0x03)])
            g.wait_ge(sem.x2, 2)
            issue([([(cid(2, chip, c), part[TB + 1])], [part[XB], part[XB + 1]], sem.tot, 0x03)])
            finish()
        return

    ranks = (cid(host, chip, 0), cid(host, chip, 4))

    if c in (0, 4):
        local(lane[XY:XY + 8], T.x[:])
        slot = 0 if c == 0 else 1
        ts = []
        for i in range(4):
            ts.append(([(cid(host, chip, H[i]), lane[HB + slot])], [lane[XY + 4 * par + i]], sem.h, 0x3 << (4 * i)))
            ts.append(([(cid(host, chip, M[i]), lane[MB + slot])], [lane[XY + 4 * (1 - par) + i]], sem.m, 0xC << (4 * i)))
        issue(ts)
        g.wait_ge(sem.d, 4 * 8 + 4 * 16)
        local(T.y[:], lane[XY:XY + 8])
        finish()
        return

    if c in M:
        i = M.index(c)
        g.wait_ge(sem.m, 4)
        issue([([(cid(host, chip ^ 1, H[i]), lane[HB + 2])], [lane[MB], lane[MB + 1]], sem.h, 0xFF)])

    if c in H:
        i = H.index(c)
        g.wait_ge(sem.h, 2 + 2 + 8)
        local(piece[HP:HP + 24], lane[HB:HB + 3])
        issue([([(cid(host, 2 * jj + par, O[i]), piece[OB + j])],
                [piece[HP + 8 * s + jj] for s in range(3)], sem.o, 1 << jj) for jj in range(8)])

    if c in O:
        i = O.index(c)
        alpha = [part[OQ + 2 * s] for s in range(8)]
        beta = [part[OQ + 2 * s + 1] for s in range(8)]
        x0, x1 = part[XB], part[XB + 1]

        def lane_receivers(ab):
            return [(cid(host, 2 * jj + par, R[i]), part[RB + 2 * j + ab]) for jj in range(8)]

        g.wait_ge(sem.o, 8)
        local(part[OQ:OQ + 16], piece[OB:OB + 8])
        if host == 0:
            issue([([(cid(1, chip, c), x0)], alpha, sem.x1, 0x03)])
            g.wait_ge(sem.x1, 2)
            issue([([(cid(3, chip, c), x1)], beta + [x0], sem.x2, 0x03)])
            g.wait_ge(sem.x2, 2)
            g.wait_ge(sem.tot, 2)
            issue([(lane_receivers(1), beta + [x0, x1], sem.r, 0x03),
                   ([(cid(1, chip, c), part[TB + 1])], beta + [x0, x1], sem.tot, 0x0C),
                   (lane_receivers(0), [part[TB]], sem.r, 0x30)])
        elif host == 1:
            issue([([(cid(0, chip, c), x0)], beta, sem.x1, 0x03)])
            g.wait_ge(sem.x1, 4)
            issue([(lane_receivers(0), alpha + [x0, x1], sem.r, 0x03),
                   ([(cid(0, chip, c), part[TB]), (cid(2, chip, c), part[TB])], alpha + [x0, x1], sem.tot, 0x0C)])
            g.wait_ge(sem.tot, 2)
            issue([(lane_receivers(1), [part[TB + 1]], sem.r, 0x03)])
        else:
            issue([([(cid(1, chip, c), x1)], alpha, sem.x1, 0x03),
                   ([(cid(3, chip, c), x0)], beta, sem.x1, 0x0C)])
            g.wait_ge(sem.tot, 4)
            issue([(lane_receivers(0), [part[TB]], sem.r, 0x03),
                   (lane_receivers(1), [part[TB + 1]], sem.r, 0x0C)])

    if c in R:
        i = R.index(c)
        g.wait_ge(sem.r, 8 * 2 * 2)
        local(lane[RL], part[RB:RB + 16])
        y = lane[XY + 4 * par + i]
        issue([([(ranks[0], y), (ranks[1], y), (cid(host, chip ^ 1, Q[i]), lane[QB])],
                [lane[RL]], sem.d, 0xFF)])

    if c in Q:
        i = Q.index(c)
        g.wait_ge(sem.d, 8)
        issue([([(r, lane[XY + 4 * (1 - par) + i]) for r in ranks], [lane[QB]], sem.d, 0xFFFF)])

    finish()
